import numpy as np
import ml_dtypes

BF16 = ml_dtypes.bfloat16


def bf(x):
    return np.asarray(x, np.float32).astype(BF16)


def f32(x):
    return np.asarray(x, np.float32)


def f64(x):
    return np.asarray(x).astype(np.float64)


def striped(idx):
    return np.tile(idx.reshape(-1, 16).T, (8, 1))


S, K, M, N, B, Q = 512, 128, 128, 512, 4, 128


def setup_inputs():
    return {"base": bf(np.random.standard_normal((B, M, S))), "x": bf(np.random.standard_normal((K, N))), "w": bf(np.random.standard_normal((K, M)) / np.sqrt(K)), "b": f32(0.5 * np.random.standard_normal((M, 1))), "offs": striped(np.random.permutation(S))}


def reference(base, x, w, b, offs):
    idx = offs[:16].T.reshape(-1)
    z = f64(base).copy()
    for i in range(B):
        z[i][:, idx[i * Q : (i + 1) * Q]] = f64(w).T @ f64(x)[:, i * Q : (i + 1) * Q]
    return np.tanh(z + f64(b))

@@ -1,0 +1,56 @@
+import concourse.mybir as mybir
+from concourse.masks import make_identity
+
+BF16, F32, U16 = mybir.dt.bfloat16, mybir.dt.float32, mybir.dt.uint16
+TANH = mybir.ActivationFunctionType.Tanh
+
+P = 128
+S = 512
+B = 4
+Q = 128
+PER_COLUMN = 16
+
+FLOPS = 2 * P * P * B * Q
+
+
+def tile_scatter_matmul_kernel(tc, base, x, w, b, offs, out):
+    nc = tc.nc
+    with (
+        tc.tile_pool(name="held", bufs=1) as held,
+        tc.psum_pool(name="psum", bufs=1) as psum,
+    ):
+        base_tiles = []
+        for i in range(B):
+            base_tile = held.tile([P, S], BF16, name=f"base{i}")
+            nc.sync.dma_start(base_tile[:], base[i])
+            base_tiles.append(base_tile)
+        x_tile = held.tile([P, B * Q], BF16, name="x_tile")
+        nc.sync.dma_start(x_tile[:], x)
+        w_tile = held.tile([P, P], BF16, name="w_tile")
+        nc.sync.dma_start(w_tile[:], w)
+        offsets = held.tile([P, B * Q // PER_COLUMN], U16, name="offsets")
+        nc.sync.dma_start(offsets[:], offs)
+        bias = held.tile([P, 1], F32, name="bias")
+        nc.sync.dma_start(bias[:], b)
+
+        identity = held.tile([P, P], BF16, name="identity")
+        make_identity(nc, identity[:])
+
+        windows = [psum.tile([P, S], F32, name=f"window{i}") for i in range(B)]
+        for i in range(B):
+            nc.tensor.matmul(windows[i][:], identity[:], base_tiles[i][:], start=True, stop=True)
+
+        k = Q // PER_COLUMN
+        for i in range(B):
+            nc.tensor.matmul(
+                windows[i][:].indirect(offsets[:, i * k : (i + 1) * k]),
+                w_tile[:],
+                x_tile[:, i * Q : (i + 1) * Q],
+                start=True,
+                stop=True,
+            )
+
+        for i in range(B):
+            result = held.tile([P, S], F32, name=f"result{i}")
+            nc.scalar.activation(result[:], windows[i][:], TANH, bias=bias[:])
+            nc.sync.dma_start(out[i], result[:])

@@ -8,6 +8,7 @@ P = 128
 S = 512
 B = 4
 Q = 128
+WARM_UPS = 4
 PER_COLUMN = 16
 
 FLOPS = 2 * P * P * B * Q
@@ -19,6 +20,11 @@ def tile_scatter_matmul_kernel(tc, base, x, w, b, offs, out):
         tc.tile_pool(name="held", bufs=1) as held,
         tc.psum_pool(name="psum", bufs=1) as psum,
     ):
+        zeros = held.tile([P, S], BF16, name="zeros")
+        nc.vector.memset(zeros[:], 0.0)
+        early = held.tile([P, 1], F32, name="early")
+        nc.scalar.activation(early[:], zeros[:, 0:1], TANH)
+
         base_tiles = []
         for i in range(B):
             base_tile = held.tile([P, S], BF16, name=f"base{i}")
@@ -35,6 +41,10 @@ def tile_scatter_matmul_kernel(tc, base, x, w, b, offs, out):
 
         identity = held.tile([P, P], BF16, name="identity")
         make_identity(nc, identity[:])
+
+        spare = psum.tile([P, S], F32, name="spare")
+        for warm in range(WARM_UPS):
+            nc.tensor.matmul(spare[:], zeros[:, 0:P], zeros[:], start=True, stop=True)
 
         windows = [psum.tile([P, S], F32, name=f"window{i}") for i in range(B)]
         for i in range(B):

@@ -8,7 +8,9 @@ P = 128
 S = 512
 B = 4
 Q = 128
-WARM_UPS = 4
+HALF = S // 2
+ZERO_COLUMNS = 256
+WARM_UPS = 6
 PER_COLUMN = 16
 
 FLOPS = 2 * P * P * B * Q
@@ -20,7 +22,7 @@ def tile_scatter_matmul_kernel(tc, base, x, w, b, offs, out):
         tc.tile_pool(name="held", bufs=1) as held,
         tc.psum_pool(name="psum", bufs=1) as psum,
     ):
-        zeros = held.tile([P, S], BF16, name="zeros")
+        zeros = held.tile([P, ZERO_COLUMNS], BF16, name="zeros")
         nc.vector.memset(zeros[:], 0.0)
         early = held.tile([P, 1], F32, name="early")
         nc.scalar.activation(early[:], zeros[:, 0:1], TANH)
@@ -42,7 +44,7 @@ def tile_scatter_matmul_kernel(tc, base, x, w, b, offs, out):
         identity = held.tile([P, P], BF16, name="identity")
         make_identity(nc, identity[:])
 
-        spare = psum.tile([P, S], F32, name="spare")
+        spare = psum.tile([P, ZERO_COLUMNS], F32, name="spare")
         for warm in range(WARM_UPS):
             nc.tensor.matmul(spare[:], zeros[:, 0:P], zeros[:], start=True, stop=True)
 
@@ -62,5 +64,7 @@ def tile_scatter_matmul_kernel(tc, base, x, w, b, offs, out):
 
         for i in range(B):
             result = held.tile([P, S], F32, name=f"result{i}")
-            nc.scalar.activation(result[:], windows[i][:], TANH, bias=bias[:])
-            nc.sync.dma_start(out[i], result[:])
+            for h in range(0, S, HALF):
+                part = slice(h, h + HALF)
+                nc.scalar.activation(result[:, part], windows[i][:, part], TANH, bias=bias[:])
+                nc.sync.dma_start(out[i, :, part], result[:, part])

import concourse.mybir as mybir
from concourse.masks import make_identity

BF16, F32, U16 = mybir.dt.bfloat16, mybir.dt.float32, mybir.dt.uint16
TANH = mybir.ActivationFunctionType.Tanh

P = 128
S = 512
B = 4
Q = 128
HALF = S // 2
ZERO_COLUMNS = 256
WARM_UPS = 6
PER_COLUMN = 16

FLOPS = 2 * P * P * B * Q


def tile_scatter_matmul_kernel(tc, base, x, w, b, offs, out):
    nc = tc.nc
    with (
        tc.tile_pool(name="held", bufs=1) as held,
        tc.psum_pool(name="psum", bufs=1) as psum,
    ):
        zeros = held.tile([P, ZERO_COLUMNS], BF16, name="zeros")
        nc.vector.memset(zeros[:], 0.0)
        early = held.tile([P, 1], F32, name="early")
        nc.scalar.activation(early[:], zeros[:, 0:1], TANH)

        base_tiles = []
        for i in range(B):
            base_tile = held.tile([P, S], BF16, name=f"base{i}")
            nc.sync.dma_start(base_tile[:], base[i])
            base_tiles.append(base_tile)
        x_tile = held.tile([P, B * Q], BF16, name="x_tile")
        nc.sync.dma_start(x_tile[:], x)
        w_tile = held.tile([P, P], BF16, name="w_tile")
        nc.sync.dma_start(w_tile[:], w)
        offsets = held.tile([P, B * Q // PER_COLUMN], U16, name="offsets")
        nc.sync.dma_start(offsets[:], offs)
        bias = held.tile([P, 1], F32, name="bias")
        nc.sync.dma_start(bias[:], b)

        identity = held.tile([P, P], BF16, name="identity")
        make_identity(nc, identity[:])

        spare = psum.tile([P, ZERO_COLUMNS], F32, name="spare")
        for warm in range(WARM_UPS):
            nc.tensor.matmul(spare[:], zeros[:, 0:P], zeros[:], start=True, stop=True)

        windows = [psum.tile([P, S], F32, name=f"window{i}") for i in range(B)]
        for i in range(B):
            nc.tensor.matmul(windows[i][:], identity[:], base_tiles[i][:], start=True, stop=True)

        k = Q // PER_COLUMN
        for i in range(B):
            nc.tensor.matmul(
                windows[i][:].indirect(offsets[:, i * k : (i + 1) * k]),
                w_tile[:],
                x_tile[:, i * Q : (i + 1) * Q],
                start=True,
                stop=True,
            )

        for i in range(B):
            result = held.tile([P, S], F32, name=f"result{i}")
            for h in range(0, S, HALF):
                part = slice(h, h + HALF)
                nc.scalar.activation(result[:, part], windows[i][:, part], TANH, bias=bias[:])
                nc.sync.dma_start(out[i, :, part], result[:, part])
